import numpy as np
import ml_dtypes


def mxq(x, axis, fmt="e4m3"):
    dtype, down = {"e4m3": (ml_dtypes.float8_e4m3fn, 7), "e5m2": (ml_dtypes.float8_e5m2, 14)}[fmt]
    v = np.moveaxis(np.asarray(x, np.float32).astype(ml_dtypes.bfloat16).astype(np.float64), axis, -1)
    blocks = v.reshape(v.shape[:-1] + (-1, 32))
    amax = np.abs(blocks).max(-1, keepdims=True)
    byte = np.maximum(np.where(amax > 0, np.frexp(amax)[1] - 1 + 127, 0) - down, 1)
    scale = np.exp2(byte - 127.0)
    codes = (blocks / scale).astype(np.float32).astype(dtype).astype(np.float64)
    return np.moveaxis((codes * scale).reshape(v.shape), -1, axis)


WIDE = False


def mx_kscale(k):
    if not WIDE:
        return np.ones(k)
    levels = np.array([10, -10, 5, -5, 0])
    if k % 512:
        return np.exp2(np.random.permutation(np.resize(levels, k // 32))).repeat(32)
    a = np.empty((k // 512, 16))
    for p in range(k // 512):
        a[p, :8] = np.random.permutation(np.resize(levels, 8))
        for g in range(8):
            far = levels[np.abs(levels - a[p, g]) >= 10]
            a[p, g + 8] = far[np.random.randint(len(far))]
    return np.exp2(a.ravel()).repeat(32)


def f64(x):
    return np.asarray(x).astype(np.float64)


def striped(idx):
    return np.tile(idx.reshape(-1, 16).T, (8, 1)).astype(np.uint16)


def unstriped(offs):
    return offs[:16].T.reshape(-1).astype(np.int64)


def striped8(idx):
    return np.concatenate([x.reshape(-1, 16).T for x in idx]).astype(np.uint16)


def runs(offs, k):
    lists = np.stack([offs[16 * r : 16 * r + 16].T.reshape(-1) for r in range(8)]).astype(np.int64)
    return lists[np.arange(k) % 512 // 64]


def pack_weight(w):
    k, n = w.shape
    w = f64(np.asarray(w, np.float32).astype(ml_dtypes.bfloat16)).reshape(k // 32, 32, n)
    amax = np.abs(w).max(1)
    byte = np.clip(np.where(amax > 0, np.frexp(amax)[1] - 1 + 127 - 7, 1), 1, 254)
    scaled = (w * np.exp2(127.0 - byte)[:, None, :]).reshape(k, n).astype(np.float32)
    words = np.ascontiguousarray(scaled.reshape(k // 512, 128, 4, n).transpose(0, 1, 3, 2)).astype(ml_dtypes.float8_e4m3fn).view(np.uint8)
    return words, np.ascontiguousarray(byte.astype(np.uint8).reshape(k // 512, 16, n))


def unpack_weight(words, scales):
    g, p, n, _ = words.shape
    vals = np.ascontiguousarray(words).view(ml_dtypes.float8_e4m3fn).astype(np.float64) * np.repeat(np.exp2(scales.astype(np.float64) - 127.0), 8, axis=1)[..., None]
    return vals.transpose(0, 1, 3, 2).reshape(g * 512, n)


K, T, S, N, H, W = 512, 2048, 512, 512, 512, 2048


def setup_inputs():
    n = np.random.standard_normal
    s = mx_kscale(K)[:, None]
    u = mx_kscale(H)
    packed_xT = pack_weight(n((K, T)) * s)
    return {
        "x_words": packed_xT[0],
        "x_scales": packed_xT[1],
        "w1": (n((K, H)) / np.sqrt(K) / s).astype(np.float32),
        "gn": (np.random.uniform(0.5, 1.5, (H, 1)) * u[:, None]).astype(np.float32),
        "w2": (n((H, N)) / np.sqrt(H) / u[:, None]).astype(np.float32),
        "offs": striped(np.random.permutation(T)[:S]),
        "n1": striped(np.random.randint(0, S, W)),
        "n2": striped8(np.stack([np.random.permutation(S) for _ in range(8)])),
        "n3": striped8(np.stack([np.random.permutation(S) for _ in range(8)])),
    }


def reference(x_words, x_scales, w1, gn, w2, offs, n1, n2, n3):
    xq = unpack_weight(x_words, x_scales)[:, unstriped(offs)]
    y = mxq(f64(w1), 0, "e4m3").T @ xq
    mb = y[:, unstriped(n1)]
    mn = mb.reshape(H, S, 4).min(axis=2)
    mx = mb.reshape(H, S, 4).max(axis=2)
    z = f64(gn) * (np.maximum(y, mn) - (0.5 * mx))
    h = mxq(f64(w2), 0, "e4m3").T @ mxq(z, 0, "e4m3")
    return h * (np.tanh(y[np.arange(H)[:, None], runs(n2, H)] - (y[np.arange(H)[:, None], runs(n3, H)])))

@@ -1,0 +1,256 @@
+from contextlib import ExitStack
+
+import concourse.mybir as mybir
+
+K, T, S, H, N = 512, 2048, 512, 512, 512
+MEMBERS = 4
+
+F32 = mybir.dt.float32
+BF16 = mybir.dt.bfloat16
+I32 = mybir.dt.int32
+U32 = mybir.dt.uint32
+U16 = mybir.dt.uint16
+U8 = mybir.dt.uint8
+FP8X4 = mybir.dt.float8_e4m3fn_x4
+ALU = mybir.AluOpType
+ACT = mybir.ActivationFunctionType
+
+P = 128
+PACK = 4
+PER_COL = 16
+HALF = S // 2
+WINDOW = 2 * S
+PIECE = 512
+
+FLOPS = 2 * K * H * S + 2 * H * N * S
+
+
+def tile_picked_skipjointbgmid_none_p_kernel(
+    tc, x_words, x_scales, w1, gn, w2, offs, n1, n2, n3, out
+):
+    nc = tc.nc
+    with ExitStack() as ctx:
+        lists = ctx.enter_context(tc.tile_pool(name="lists", bufs=1))
+        keep = ctx.enter_context(tc.tile_pool(name="keep", bufs=1))
+        ring = ctx.enter_context(tc.tile_pool(name="ring", bufs=3))
+        psum = ctx.enter_context(tc.psum_pool(name="psum", bufs=1))
+
+        def load_list(name, src):
+            tile = lists.tile(list(src.shape), U16, name=name)
+            nc.sync.dma_start(tile[:], src)
+            return tile
+
+        def load_weight(name, src):
+            tile = keep.tile([P, PACK, src.shape[1]], F32, name=name)
+            nc.sync.dma_start(tile[:], src.rearrange("(p j) c -> p j c", j=PACK))
+            return tile
+
+        scale_table = keep.tile([P, T], U8, name="scale_table", align_bytes=64)
+        nc.vector.memset(scale_table[:].bitcast(I32), 0)
+        offs_sb = load_list("offs_sb", offs)
+        w1_raw = load_weight("w1_raw", w1)
+        word_table = keep.tile([P, T], I32, name="word_table", align_bytes=64)
+        nc.sync.dma_start(word_table[:], x_words[0].rearrange("p n t -> p (n t)").bitcast(I32))
+        for q in range(4):
+            nc.scalar.dma_start(
+                scale_table[32 * q : 32 * q + 4, :].bitcast(I32),
+                x_scales[0, 4 * q : 4 * q + 4, :].bitcast(I32),
+            )
+        n1_sb = load_list("n1_sb", n1)
+        w2_raw = load_weight("w2_raw", w2)
+        gain = keep.tile([P, PACK], F32, name="gain")
+        nc.sync.dma_start(gain[:], gn.rearrange("(p t) o -> p (t o)", t=PACK))
+        n2_sb = load_list("n2_sb", n2)
+        n3_sb = load_list("n3_sb", n3)
+
+        y = [keep.tile([P, WINDOW], F32, name="y%d" % t) for t in range(PACK)]
+        for t in range(PACK):
+            nc.vector.memset(y[t][:, S:], 0.0)
+
+        x_bytes = keep.tile([P, S], U8, name="x_bytes", align_bytes=64)
+        nc.vector.tensor_copy(x_bytes[:], scale_table[:].indirect(offs_sb[:]))
+
+        w1_codes = keep.tile([P, H], U32, name="w1_codes", align_bytes=64)
+        w1_bytes = keep.tile([P, H], U8, name="w1_bytes", align_bytes=64)
+        w1_view = w1_raw[:].rearrange("p j (m t) -> p m j t", t=PACK)
+        w1_pairs = []
+        for u in range(2):
+            pair = keep.tile([P, 2, P, PACK], BF16, name="w1_pair%d" % u, align_bytes=64)
+            dst = pair[:].rearrange("p t m j -> p m j t")
+            src = w1_view[:, :, :, 2 * u : 2 * u + 2]
+            if u == 0:
+                nc.vector.tensor_copy(dst, src)
+            else:
+                nc.scalar.activation(dst, src, ACT.Copy)
+            w1_pairs.append(pair)
+        for u in range(2):
+            cols = slice(2 * P * u, 2 * P * (u + 1))
+            nc.vector.quantize_mx(
+                out=w1_codes[:, cols].bitcast(FP8X4),
+                scales=w1_bytes[:, cols],
+                in_=w1_pairs[u][:].rearrange("p t m j -> p (t m j)"),
+            )
+
+        x_codes = keep.tile([P, S], U32, name="x_codes", align_bytes=64)
+        for h in range(2):
+            nc.vector.tensor_copy(
+                x_codes[:, HALF * h : HALF * (h + 1)],
+                word_table[:].bitcast(U32).indirect(offs_sb[:, HALF // PER_COL * h : HALF // PER_COL * (h + 1)]),
+            )
+
+        def product(bank, codes, scales, t, rhs_codes, rhs_scales):
+            rows = slice(P * t, P * (t + 1))
+            nc.tensor.matmul_mx(
+                out=bank,
+                lhsT=codes[:, rows].bitcast(FP8X4),
+                lhsT_scale=scales[:, rows],
+                rhs=rhs_codes.bitcast(FP8X4),
+                rhs_scale=rhs_scales,
+                start=True,
+                stop=True,
+            )
+
+        for h in range(2):
+            cols = slice(HALF * h, HALF * (h + 1))
+            bank = psum.tile([P, HALF], F32, name="first%d" % h, tag="bank%d" % h)
+            product(bank[:], w1_codes, w1_bytes, 0, x_codes[:, cols], x_bytes[:, cols])
+            nc.scalar.activation(y[0][:, cols], bank[:], ACT.Copy)
+        for t in range(1, PACK):
+            bank = psum.tile([P, S], F32, name="ybank%d" % t, tag="bank%d" % (t + 1))
+            product(bank[:], w1_codes, w1_bytes, t, x_codes[:], x_bytes[:])
+            nc.vector.tensor_copy(y[t][:, :S], bank[:])
+
+        w2_grouped = keep.tile([P, PACK, P, PACK], BF16, name="w2_grouped", align_bytes=64)
+        nc.vector.tensor_copy(
+            w2_grouped[:].rearrange("p t m j -> p m j t"),
+            w2_raw[:].rearrange("p j (m t) -> p m j t", t=PACK),
+        )
+        w2_codes = keep.tile([P, N], U32, name="w2_codes", align_bytes=64)
+        w2_bytes = keep.tile([P, N], U8, name="w2_bytes", align_bytes=64)
+
+        def quantize_w2():
+            nc.vector.quantize_mx(
+                out=w2_codes[:].bitcast(FP8X4),
+                scales=w2_bytes[:],
+                in_=w2_grouped[:].rearrange("p t m j -> p (t m j)"),
+            )
+
+        units = [(h, t) for h in range(2) for t in range(PACK)]
+        members = {}
+        for h, t in units:
+            mb = keep.tile([P, HALF, MEMBERS], F32, name="mb%d_%d" % (h, t))
+            flat = mb[:].rearrange("p c e -> p (c e)")
+            for i in range(HALF * MEMBERS // PIECE):
+                first = HALF * MEMBERS * h + PIECE * i
+                nc.scalar.activation(
+                    flat[:, PIECE * i : PIECE * (i + 1)],
+                    y[t][:].indirect(n1_sb[:, first // PER_COL : (first + PIECE) // PER_COL]),
+                    ACT.Copy,
+                )
+            members[h, t] = mb
+
+        at_n2, at_n3 = [], []
+        for t in range(PACK):
+            g2 = keep.tile([P, S], F32, name="g2_%d" % t)
+            g3 = keep.tile([P, S], F32, name="g3_%d" % t)
+            nc.scalar.activation(g2[:], y[t][:].indirect(n2_sb[:]), ACT.Copy)
+            nc.scalar.activation(g3[:], y[t][:].indirect(n3_sb[:]), ACT.Copy)
+            at_n2.append(g2)
+            at_n3.append(g3)
+
+        z_planes = [keep.tile([P, PACK, HALF], BF16, name="z_planes%d" % h) for h in range(2)]
+        z_grouped = [keep.tile([P, HALF, PACK], BF16, name="z_grouped%d" % h, align_bytes=64) for h in range(2)]
+        z_codes = [keep.tile([P, HALF], U32, name="z_codes%d" % h, align_bytes=64) for h in range(2)]
+        z_bytes = [keep.tile([P, HALF], U8, name="z_bytes%d" % h, align_bytes=64) for h in range(2)]
+        h_tags = ["bank5", "bank6", "bank7", "bank0"]
+        h_banks = [psum.tile([P, S], F32, name="hbank%d" % t, tag=h_tags[t]) for t in range(PACK)]
+        state = {}
+
+        def pair_step(unit, op, tag):
+            mb = members[unit]
+            res = ring.tile([P, HALF, 2], F32, name=tag)
+            nc.vector.tensor_tensor(res[:], mb[:, :, 0:2], mb[:, :, 2:4], op)
+            state[unit, tag] = res
+
+        def last_step(unit, op, src_tag, tag):
+            two = state[unit, src_tag]
+            res = ring.tile([P, HALF], F32, name=tag)
+            nc.vector.tensor_tensor(res[:], two[:, :, 0], two[:, :, 1], op)
+            state[unit, tag] = res
+
+        def larger(unit):
+            h, t = unit
+            res = ring.tile([P, HALF], F32, name="big")
+            nc.vector.tensor_tensor(res[:], y[t][:, HALF * h : HALF * (h + 1)], state[unit, "mn"][:], ALU.max)
+            state[unit, "big"] = res
+
+        def less_half(unit):
+            res = ring.tile([P, HALF], F32, name="pre")
+            nc.vector.scalar_tensor_tensor(
+                res[:], state[unit, "mx"][:], -0.5, state[unit, "big"][:], ALU.mult, ALU.add
+            )
+            state[unit, "pre"] = res
+
+        def gained(unit):
+            h, t = unit
+            nc.vector.tensor_scalar(
+                z_planes[h][:, t, :], state[unit, "pre"][:], gain[:, t : t + 1], None, ALU.mult
+            )
+
+        def interleave(h):
+            nc.vector.tensor_copy(
+                z_grouped[h][:].rearrange("p (c i) t -> p c t i", i=4),
+                z_planes[h][:].rearrange("p t (c i) -> p c t i", i=4),
+            )
+
+        def second_product(h):
+            nc.vector.quantize_mx(
+                out=z_codes[h][:].bitcast(FP8X4),
+                scales=z_bytes[h][:],
+                in_=z_grouped[h][:].rearrange("p c t -> p (c t)"),
+            )
+            for t in range(PACK):
+                product(h_banks[t][:, HALF * h : HALF * (h + 1)], w2_codes, w2_bytes, t, z_codes[h][:], z_bytes[h][:])
+
+        diffs = []
+
+        def difference(t):
+            d = keep.tile([P, S], F32, name="diff%d" % t)
+            nc.vector.tensor_tensor(d[:], at_n2[t][:], at_n3[t][:], ALU.subtract)
+            diffs.append(d)
+
+        before = None
+        for i, unit in enumerate(units):
+            pair_step(unit, ALU.min, "lo")
+            if before is None:
+                quantize_w2()
+            else:
+                less_half(before)
+            pair_step(unit, ALU.max, "hi")
+            if before is not None:
+                gained(before)
+            last_step(unit, ALU.min, "lo", "mn")
+            if i == PACK:
+                interleave(0)
+            last_step(unit, ALU.max, "hi", "mx")
+            if i == PACK:
+                second_product(0)
+            larger(unit)
+            before = unit
+        difference(0)
+        less_half(before)
+        difference(1)
+        gained(before)
+        interleave(1)
+        difference(2)
+        second_product(1)
+        difference(3)
+
+        out_rows = out.rearrange("(p t) n -> p t n", t=PACK)
+        spans = [(t, 0, S) for t in range(PACK - 1)] + [(PACK - 1, 0, HALF), (PACK - 1, HALF, S)]
+        for t, a, b in spans:
+            gate = keep.tile([P, b - a], F32, name="gate%d_%d" % (t, a))
+            nc.scalar.activation(gate[:], diffs[t][:, a:b], ACT.Tanh)
+            res = keep.tile([P, b - a], F32, name="res%d_%d" % (t, a))
+            nc.vector.tensor_tensor(res[:], h_banks[t][:, a:b], gate[:], ALU.mult)
+            nc.sync.dma_start(out_rows[:, t, a:b], res[:])

@@ -19,8 +19,8 @@ P = 128
 PACK = 4
 PER_COL = 16
 HALF = S // 2
-WINDOW = 2 * S
-PIECE = 512
+PIECE = 1024
+WINDOW = PIECE + PER_COL
 
 FLOPS = 2 * K * H * S + 2 * H * N * S
 
@@ -32,7 +32,7 @@ def tile_picked_skipjointbgmid_none_p_kernel(
     with ExitStack() as ctx:
         lists = ctx.enter_context(tc.tile_pool(name="lists", bufs=1))
         keep = ctx.enter_context(tc.tile_pool(name="keep", bufs=1))
-        ring = ctx.enter_context(tc.tile_pool(name="ring", bufs=3))
+        ring = ctx.enter_context(tc.tile_pool(name="ring", bufs=2))
         psum = ctx.enter_context(tc.psum_pool(name="psum", bufs=1))
 
         def load_list(name, src):
@@ -49,14 +49,14 @@ def tile_picked_skipjointbgmid_none_p_kernel(
         nc.vector.memset(scale_table[:].bitcast(I32), 0)
         offs_sb = load_list("offs_sb", offs)
         w1_raw = load_weight("w1_raw", w1)
-        word_table = keep.tile([P, T], I32, name="word_table", align_bytes=64)
-        nc.sync.dma_start(word_table[:], x_words[0].rearrange("p n t -> p (n t)").bitcast(I32))
+        n1_sb = load_list("n1_sb", n1)
         for q in range(4):
-            nc.scalar.dma_start(
+            nc.sync.dma_start(
                 scale_table[32 * q : 32 * q + 4, :].bitcast(I32),
                 x_scales[0, 4 * q : 4 * q + 4, :].bitcast(I32),
             )
-        n1_sb = load_list("n1_sb", n1)
+        word_table = keep.tile([P, T], I32, name="word_table", align_bytes=64)
+        nc.sync.dma_start(word_table[:], x_words[0].rearrange("p n t -> p (n t)").bitcast(I32))
         w2_raw = load_weight("w2_raw", w2)
         gain = keep.tile([P, PACK], F32, name="gain")
         nc.sync.dma_start(gain[:], gn.rearrange("(p t) o -> p (t o)", t=PACK))
@@ -135,122 +135,100 @@ def tile_picked_skipjointbgmid_none_p_kernel(
                 in_=w2_grouped[:].rearrange("p t m j -> p (t m j)"),
             )
 
-        units = [(h, t) for h in range(2) for t in range(PACK)]
-        members = {}
-        for h, t in units:
-            mb = keep.tile([P, HALF, MEMBERS], F32, name="mb%d_%d" % (h, t))
+        members = []
+        for t in range(PACK):
+            mb = keep.tile([P, S, MEMBERS], F32, name="mb%d" % t)
             flat = mb[:].rearrange("p c e -> p (c e)")
-            for i in range(HALF * MEMBERS // PIECE):
-                first = HALF * MEMBERS * h + PIECE * i
+            for first in range(0, S * MEMBERS, PIECE):
                 nc.scalar.activation(
-                    flat[:, PIECE * i : PIECE * (i + 1)],
+                    flat[:, first : first + PIECE],
                     y[t][:].indirect(n1_sb[:, first // PER_COL : (first + PIECE) // PER_COL]),
                     ACT.Copy,
                 )
-            members[h, t] = mb
+            members.append(mb)
 
-        at_n2, at_n3 = [], []
-        for t in range(PACK):
-            g2 = keep.tile([P, S], F32, name="g2_%d" % t)
-            g3 = keep.tile([P, S], F32, name="g3_%d" % t)
-            nc.scalar.activation(g2[:], y[t][:].indirect(n2_sb[:]), ACT.Copy)
-            nc.scalar.activation(g3[:], y[t][:].indirect(n3_sb[:]), ACT.Copy)
-            at_n2.append(g2)
-            at_n3.append(g3)
-
-        z_planes = [keep.tile([P, PACK, HALF], BF16, name="z_planes%d" % h) for h in range(2)]
-        z_grouped = [keep.tile([P, HALF, PACK], BF16, name="z_grouped%d" % h, align_bytes=64) for h in range(2)]
-        z_codes = [keep.tile([P, HALF], U32, name="z_codes%d" % h, align_bytes=64) for h in range(2)]
-        z_bytes = [keep.tile([P, HALF], U8, name="z_bytes%d" % h, align_bytes=64) for h in range(2)]
+        z_planes = keep.tile([P, PACK, S], BF16, name="z_planes")
+        z_grouped = keep.tile([P, S, PACK], BF16, name="z_grouped", align_bytes=64)
+        z_codes = keep.tile([P, S], U32, name="z_codes", align_bytes=64)
+        z_bytes = keep.tile([P, S], U8, name="z_bytes", align_bytes=64)
         h_tags = ["bank5", "bank6", "bank7", "bank0"]
         h_banks = [psum.tile([P, S], F32, name="hbank%d" % t, tag=h_tags[t]) for t in range(PACK)]
-        state = {}
+        lows = [keep.tile([P, S, 2], F32, name="low%d" % t) for t in range(PACK)]
+        highs = [keep.tile([P, S, 2], F32, name="high%d" % t) for t in range(PACK)]
+        smallest = [keep.tile([P, S], F32, name="smallest%d" % t) for t in range(PACK)]
+        largest = [keep.tile([P, S], F32, name="largest%d" % t) for t in range(PACK)]
+        larger = [keep.tile([P, S], F32, name="larger%d" % t) for t in range(PACK)]
+        ungained = [keep.tile([P, S], F32, name="ungained%d" % t) for t in range(PACK)]
 
-        def pair_step(unit, op, tag):
-            mb = members[unit]
-            res = ring.tile([P, HALF, 2], F32, name=tag)
-            nc.vector.tensor_tensor(res[:], mb[:, :, 0:2], mb[:, :, 2:4], op)
-            state[unit, tag] = res
+        def pair_step(t, h, pairs, op):
+            cols = slice(HALF * h, HALF * (h + 1))
+            nc.vector.tensor_tensor(pairs[t][:, cols, :], members[t][:, cols, 0:2], members[t][:, cols, 2:4], op)
 
-        def last_step(unit, op, src_tag, tag):
-            two = state[unit, src_tag]
-            res = ring.tile([P, HALF], F32, name=tag)
-            nc.vector.tensor_tensor(res[:], two[:, :, 0], two[:, :, 1], op)
-            state[unit, tag] = res
+        def less_half(t):
+            nc.vector.scalar_tensor_tensor(ungained[t][:], largest[t][:], -0.5, larger[t][:], ALU.mult, ALU.add)
 
-        def larger(unit):
-            h, t = unit
-            res = ring.tile([P, HALF], F32, name="big")
-            nc.vector.tensor_tensor(res[:], y[t][:, HALF * h : HALF * (h + 1)], state[unit, "mn"][:], ALU.max)
-            state[unit, "big"] = res
-
-        def less_half(unit):
-            res = ring.tile([P, HALF], F32, name="pre")
-            nc.vector.scalar_tensor_tensor(
-                res[:], state[unit, "mx"][:], -0.5, state[unit, "big"][:], ALU.mult, ALU.add
-            )
-            state[unit, "pre"] = res
-
-        def gained(unit):
-            h, t = unit
-            nc.vector.tensor_scalar(
-                z_planes[h][:, t, :], state[unit, "pre"][:], gain[:, t : t + 1], None, ALU.mult
-            )
-
-        def interleave(h):
-            nc.vector.tensor_copy(
-                z_grouped[h][:].rearrange("p (c i) t -> p c t i", i=4),
-                z_planes[h][:].rearrange("p t (c i) -> p c t i", i=4),
-            )
-
-        def second_product(h):
-            nc.vector.quantize_mx(
-                out=z_codes[h][:].bitcast(FP8X4),
-                scales=z_bytes[h][:],
-                in_=z_grouped[h][:].rearrange("p c t -> p (c t)"),
-            )
-            for t in range(PACK):
-                product(h_banks[t][:, HALF * h : HALF * (h + 1)], w2_codes, w2_bytes, t, z_codes[h][:], z_bytes[h][:])
-
-        diffs = []
-
-        def difference(t):
-            d = keep.tile([P, S], F32, name="diff%d" % t)
-            nc.vector.tensor_tensor(d[:], at_n2[t][:], at_n3[t][:], ALU.subtract)
-            diffs.append(d)
-
-        before = None
-        for i, unit in enumerate(units):
-            pair_step(unit, ALU.min, "lo")
-            if before is None:
-                quantize_w2()
-            else:
-                less_half(before)
-            pair_step(unit, ALU.max, "hi")
-            if before is not None:
-                gained(before)
-            last_step(unit, ALU.min, "lo", "mn")
-            if i == PACK:
-                interleave(0)
-            last_step(unit, ALU.max, "hi", "mx")
-            if i == PACK:
-                second_product(0)
-            larger(unit)
-            before = unit
-        difference(0)
-        less_half(before)
-        difference(1)
-        gained(before)
-        interleave(1)
-        difference(2)
-        second_product(1)
-        difference(3)
+        def gained(t):
+            nc.vector.tensor_scalar(z_planes[:, t, :], ungained[t][:], gain[:, t : t + 1], None, ALU.mult)
 
         out_rows = out.rearrange("(p t) n -> p t n", t=PACK)
-        spans = [(t, 0, S) for t in range(PACK - 1)] + [(PACK - 1, 0, HALF), (PACK - 1, HALF, S)]
-        for t, a, b in spans:
+        diffs, gates = {}, {}
+
+        def difference(t):
+            g2 = ring.tile([P, S], F32, name="g2")
+            g3 = ring.tile([P, S], F32, name="g3")
+            nc.scalar.activation(g2[:], y[t][:].indirect(n2_sb[:]), ACT.Copy)
+            nc.scalar.activation(g3[:], y[t][:].indirect(n3_sb[:]), ACT.Copy)
+            nc.vector.tensor_tensor(g2[:], g2[:], g3[:], ALU.subtract)
+            diffs[t] = g2
+
+        def make_gate(t, a, b):
             gate = keep.tile([P, b - a], F32, name="gate%d_%d" % (t, a))
             nc.scalar.activation(gate[:], diffs[t][:, a:b], ACT.Tanh)
+            gates[t, a] = gate
+
+        def finish(t, a, b):
             res = keep.tile([P, b - a], F32, name="res%d_%d" % (t, a))
-            nc.vector.tensor_tensor(res[:], h_banks[t][:, a:b], gate[:], ALU.mult)
+            nc.vector.tensor_tensor(res[:], h_banks[t][:, a:b], gates[t, a][:], ALU.mult)
             nc.sync.dma_start(out_rows[:, t, a:b], res[:])
+
+        for t in range(PACK):
+            pair_step(t, 0, lows, ALU.min)
+            if t == 0:
+                quantize_w2()
+            else:
+                less_half(t - 1)
+            pair_step(t, 0, highs, ALU.max)
+            if t > 0:
+                gained(t - 1)
+            pair_step(t, 1, lows, ALU.min)
+            pair_step(t, 1, highs, ALU.max)
+            nc.vector.tensor_tensor(smallest[t][:], lows[t][:, :, 0], lows[t][:, :, 1], ALU.min)
+            nc.vector.tensor_tensor(largest[t][:], highs[t][:, :, 0], highs[t][:, :, 1], ALU.max)
+            nc.vector.tensor_tensor(larger[t][:], y[t][:, :S], smallest[t][:], ALU.max)
+        last = PACK - 1
+        difference(0)
+        less_half(last)
+        gained(last)
+        nc.vector.tensor_copy(
+            z_grouped[:].rearrange("p (c i) t -> p c t i", i=4),
+            z_planes[:].rearrange("p t (c i) -> p c t i", i=4),
+        )
+        difference(1)
+        make_gate(0, 0, S)
+        nc.vector.quantize_mx(
+            out=z_codes[:].bitcast(FP8X4),
+            scales=z_bytes[:],
+            in_=z_grouped[:].rearrange("p c t -> p (c t)"),
+        )
+        for t in range(PACK):
+            product(h_banks[t][:], w2_codes, w2_bytes, t, z_codes[:], z_bytes[:])
+        difference(2)
+        make_gate(1, 0, S)
+        finish(0, 0, S)
+        finish(1, 0, S)
+        difference(3)
+        make_gate(2, 0, S)
+        finish(2, 0, S)
+        for a in (0, HALF):
+            make_gate(last, a, a + HALF)
+            finish(last, a, a + HALF)

@@ -1,6 +1,7 @@
 from contextlib import ExitStack
 
 import concourse.mybir as mybir
+from concourse.masks import make_identity
 
 K, T, S, H, N = 512, 2048, 512, 512, 512
 MEMBERS = 4
@@ -32,7 +33,7 @@ def tile_picked_skipjointbgmid_none_p_kernel(
     with ExitStack() as ctx:
         lists = ctx.enter_context(tc.tile_pool(name="lists", bufs=1))
         keep = ctx.enter_context(tc.tile_pool(name="keep", bufs=1))
-        ring = ctx.enter_context(tc.tile_pool(name="ring", bufs=2))
+        ring = ctx.enter_context(tc.tile_pool(name="ring", bufs=3))
         psum = ctx.enter_context(tc.psum_pool(name="psum", bufs=1))
 
         def load_list(name, src):
@@ -47,9 +48,10 @@ def tile_picked_skipjointbgmid_none_p_kernel(
 
         scale_table = keep.tile([P, T], U8, name="scale_table", align_bytes=64)
         nc.vector.memset(scale_table[:].bitcast(I32), 0)
-        offs_sb = load_list("offs_sb", offs)
         w1_raw = load_weight("w1_raw", w1)
-        n1_sb = load_list("n1_sb", n1)
+        offs_sb = load_list("offs_sb", offs)
+        gain = keep.tile([P, PACK], F32, name="gain")
+        nc.sync.dma_start(gain[:], gn.rearrange("(p t) o -> p (t o)", t=PACK))
         for q in range(4):
             nc.sync.dma_start(
                 scale_table[32 * q : 32 * q + 4, :].bitcast(I32),
@@ -57,15 +59,22 @@ def tile_picked_skipjointbgmid_none_p_kernel(
             )
         word_table = keep.tile([P, T], I32, name="word_table", align_bytes=64)
         nc.sync.dma_start(word_table[:], x_words[0].rearrange("p n t -> p (n t)").bitcast(I32))
+        n1_sb = load_list("n1_sb", n1)
         w2_raw = load_weight("w2_raw", w2)
-        gain = keep.tile([P, PACK], F32, name="gain")
-        nc.sync.dma_start(gain[:], gn.rearrange("(p t) o -> p (t o)", t=PACK))
         n2_sb = load_list("n2_sb", n2)
         n3_sb = load_list("n3_sb", n3)
 
         y = [keep.tile([P, WINDOW], F32, name="y%d" % t) for t in range(PACK)]
         for t in range(PACK):
             nc.vector.memset(y[t][:, S:], 0.0)
+
+        ident = keep.tile([P, P], F32, name="ident")
+        make_identity(nc, ident[:])
+        gain_bank = psum.tile([P, PACK, P], F32, name="gain_bank", tag="bank5")
+        for t in range(PACK):
+            nc.tensor.transpose(gain_bank[:, t, :], gain[:, t : t + 1].to_broadcast([P, P]), ident[:])
+        gain_row = keep.tile([P, 2, P, 2], F32, name="gain_row")
+        nc.scalar.activation(gain_row[:], gain_bank[:].rearrange("j (u e) p -> j u p e", e=2), ACT.Copy)
 
         x_bytes = keep.tile([P, S], U8, name="x_bytes", align_bytes=64)
         nc.vector.tensor_copy(x_bytes[:], scale_table[:].indirect(offs_sb[:]))
@@ -135,51 +144,96 @@ def tile_picked_skipjointbgmid_none_p_kernel(
                 in_=w2_grouped[:].rearrange("p t m j -> p (t m j)"),
             )
 
-        members = []
-        for t in range(PACK):
-            mb = keep.tile([P, S, MEMBERS], F32, name="mb%d" % t)
-            flat = mb[:].rearrange("p c e -> p (c e)")
-            for first in range(0, S * MEMBERS, PIECE):
+        members = {}
+        for h in range(2):
+            for t in range(PACK):
+                mb = keep.tile([P, HALF, MEMBERS], F32, name="mb%d_%d" % (h, t))
                 nc.scalar.activation(
-                    flat[:, first : first + PIECE],
-                    y[t][:].indirect(n1_sb[:, first // PER_COL : (first + PIECE) // PER_COL]),
+                    mb[:].rearrange("p c e -> p (c e)"),
+                    y[t][:].indirect(n1_sb[:, PIECE // PER_COL * h : PIECE // PER_COL * (h + 1)]),
                     ACT.Copy,
+                    scale=-0.5,
                 )
-            members.append(mb)
+                members[h, t] = mb
 
-        z_planes = keep.tile([P, PACK, S], BF16, name="z_planes")
-        z_grouped = keep.tile([P, S, PACK], BF16, name="z_grouped", align_bytes=64)
-        z_codes = keep.tile([P, S], U32, name="z_codes", align_bytes=64)
-        z_bytes = keep.tile([P, S], U8, name="z_bytes", align_bytes=64)
-        h_tags = ["bank5", "bank6", "bank7", "bank0"]
-        h_banks = [psum.tile([P, S], F32, name="hbank%d" % t, tag=h_tags[t]) for t in range(PACK)]
-        lows = [keep.tile([P, S, 2], F32, name="low%d" % t) for t in range(PACK)]
-        highs = [keep.tile([P, S, 2], F32, name="high%d" % t) for t in range(PACK)]
-        smallest = [keep.tile([P, S], F32, name="smallest%d" % t) for t in range(PACK)]
-        largest = [keep.tile([P, S], F32, name="largest%d" % t) for t in range(PACK)]
-        larger = [keep.tile([P, S], F32, name="larger%d" % t) for t in range(PACK)]
-        ungained = [keep.tile([P, S], F32, name="ungained%d" % t) for t in range(PACK)]
+        units = [(h, u) for h in range(2) for u in range(2)]
+        lows = {k: keep.tile([P, 2, HALF, 2], F32, name="low%d_%d" % k) for k in units}
+        highs = {k: keep.tile([P, 2, HALF, 2], F32, name="high%d_%d" % k) for k in units}
+        smallest = {k: keep.tile([P, 2, HALF], F32, name="smallest%d_%d" % k) for k in units}
+        largest = {k: keep.tile([P, 2, HALF], F32, name="largest%d_%d" % k) for k in units}
+        larger = {k: keep.tile([P, 2, HALF], F32, name="larger%d_%d" % k) for k in units}
+        sum_tags = ["bank5", "bank6", "bank7", "bank0"]
+        sum_banks, word_banks, h_banks = {}, {}, {}
+        z_turned = [keep.tile([P, 2, P, 2], BF16, name="z_turned%d" % b) for b in range(4)]
+        z_grouped = [keep.tile([P, HALF, PACK], BF16, name="z_grouped%d" % h, align_bytes=64) for h in range(2)]
+        z_codes = [keep.tile([P, HALF], U32, name="z_codes%d" % h, align_bytes=64) for h in range(2)]
+        z_bytes = [keep.tile([P, HALF], U8, name="z_bytes%d" % h, align_bytes=64) for h in range(2)]
 
-        def pair_step(t, h, pairs, op):
-            cols = slice(HALF * h, HALF * (h + 1))
-            nc.vector.tensor_tensor(pairs[t][:, cols, :], members[t][:, cols, 0:2], members[t][:, cols, 2:4], op)
+        def pair_step(h, t):
+            mb = members[h, t]
+            k, e = (h, t // 2), t % 2
+            nc.vector.tensor_tensor(highs[k][:, e], mb[:, :, 0:2], mb[:, :, 2:4], ALU.max)
+            nc.vector.tensor_tensor(lows[k][:, e], mb[:, :, 0:2], mb[:, :, 2:4], ALU.min)
 
-        def less_half(t):
-            nc.vector.scalar_tensor_tensor(ungained[t][:], largest[t][:], -0.5, larger[t][:], ALU.mult, ALU.add)
+        def extremes(k):
+            nc.vector.tensor_tensor(largest[k][:], highs[k][:, :, :, 0], highs[k][:, :, :, 1], ALU.max)
+            nc.vector.tensor_tensor(smallest[k][:], lows[k][:, :, :, 0], lows[k][:, :, :, 1], ALU.min)
 
-        def gained(t):
-            nc.vector.tensor_scalar(z_planes[:, t, :], ungained[t][:], gain[:, t : t + 1], None, ALU.mult)
+        def turn_sums(k):
+            h, u = k
+            if u == 0:
+                for b in (2 * h, 2 * h + 1):
+                    sum_banks[b] = psum.tile([P, PACK, P], F32, name="sum_bank%d" % b, tag=sum_tags[b])
+            for e in range(2):
+                t = 2 * u + e
+                nc.vector.scalar_tensor_tensor(
+                    larger[k][:, e], largest[k][:, e], -2.0, y[t][:, HALF * h : HALF * (h + 1)], ALU.mult, ALU.max
+                )
+                for b in range(2):
+                    cols = slice(P * b, P * (b + 1))
+                    dst = sum_banks[2 * h + b][:, t, :]
+                    nc.tensor.matmul(dst, smallest[k][:, e, cols], ident[:], start=True, stop=False, is_transpose=True)
+                    nc.tensor.matmul(dst, larger[k][:, e, cols], ident[:], start=False, stop=True, is_transpose=True)
+
+        def gain_and_turn_back(h):
+            word_banks[h] = psum.tile([P, 2, 2, P], F32, name="word_bank%d" % h, tag="bank%d" % (1 + h))
+            for b in range(2):
+                zt = z_turned[2 * h + b]
+                nc.vector.tensor_tensor(
+                    zt[:], sum_banks[2 * h + b][:].rearrange("j (u e) p -> j u p e", e=2), gain_row[:], ALU.mult
+                )
+                words = zt[:].rearrange("j u p e -> j (u p e)").bitcast(F32)
+                for u in range(2):
+                    nc.tensor.transpose(word_banks[h][:, b, u, :], words[:, P * u : P * (u + 1)], ident[:])
+
+        def group_z(h):
+            nc.vector.tensor_copy(
+                z_grouped[h][:].rearrange("p c t -> p (c t)").bitcast(F32).rearrange("p (b j u) -> p b j u", b=2, u=2),
+                word_banks[h][:].rearrange("p b u j -> p b j u"),
+            )
+
+        def second_product(h):
+            nc.vector.quantize_mx(
+                out=z_codes[h][:].bitcast(FP8X4),
+                scales=z_bytes[h][:],
+                in_=z_grouped[h][:].rearrange("p c t -> p (c t)"),
+            )
+            for t in range(PACK):
+                if h == 0:
+                    h_banks[t] = psum.tile([P, S], F32, name="hbank%d" % t, tag="bank%d" % (3 + t))
+                product(h_banks[t][:, HALF * h : HALF * (h + 1)], w2_codes, w2_bytes, t, z_codes[h][:], z_bytes[h][:])
 
         out_rows = out.rearrange("(p t) n -> p t n", t=PACK)
         diffs, gates = {}, {}
 
-        def difference(t):
+        def difference(t, engine):
             g2 = ring.tile([P, S], F32, name="g2")
             g3 = ring.tile([P, S], F32, name="g3")
             nc.scalar.activation(g2[:], y[t][:].indirect(n2_sb[:]), ACT.Copy)
             nc.scalar.activation(g3[:], y[t][:].indirect(n3_sb[:]), ACT.Copy)
-            nc.vector.tensor_tensor(g2[:], g2[:], g3[:], ALU.subtract)
-            diffs[t] = g2
+            dst = g2[:] if t < 2 else late_diffs[:, t - 2, :]
+            engine.tensor_tensor(dst, g2[:], g3[:], ALU.subtract)
+            diffs[t] = dst
 
         def make_gate(t, a, b):
             gate = keep.tile([P, b - a], F32, name="gate%d_%d" % (t, a))
@@ -191,44 +245,41 @@ def tile_picked_skipjointbgmid_none_p_kernel(
             nc.vector.tensor_tensor(res[:], h_banks[t][:, a:b], gates[t, a][:], ALU.mult)
             nc.sync.dma_start(out_rows[:, t, a:b], res[:])
 
-        for t in range(PACK):
-            pair_step(t, 0, lows, ALU.min)
-            if t == 0:
-                quantize_w2()
-            else:
-                less_half(t - 1)
-            pair_step(t, 0, highs, ALU.max)
-            if t > 0:
-                gained(t - 1)
-            pair_step(t, 1, lows, ALU.min)
-            pair_step(t, 1, highs, ALU.max)
-            nc.vector.tensor_tensor(smallest[t][:], lows[t][:, :, 0], lows[t][:, :, 1], ALU.min)
-            nc.vector.tensor_tensor(largest[t][:], highs[t][:, :, 0], highs[t][:, :, 1], ALU.max)
-            nc.vector.tensor_tensor(larger[t][:], y[t][:, :S], smallest[t][:], ALU.max)
-        last = PACK - 1
-        difference(0)
-        less_half(last)
-        gained(last)
-        nc.vector.tensor_copy(
-            z_grouped[:].rearrange("p (c i) t -> p c t i", i=4),
-            z_planes[:].rearrange("p t (c i) -> p c t i", i=4),
-        )
-        difference(1)
+        pair_step(0, 0)
+        quantize_w2()
+        pair_step(0, 1)
+        extremes((0, 0))
+        turn_sums((0, 0))
+        pair_step(0, 2)
+        pair_step(0, 3)
+        extremes((0, 1))
+        turn_sums((0, 1))
+        pair_step(1, 0)
+        gain_and_turn_back(0)
+        pair_step(1, 1)
+        group_z(0)
+        extremes((1, 0))
+        second_product(0)
+        turn_sums((1, 0))
+        pair_step(1, 2)
+        pair_step(1, 3)
+        extremes((1, 1))
+        turn_sums((1, 1))
+        difference(0, nc.vector)
+        gain_and_turn_back(1)
+        difference(1, nc.vector)
         make_gate(0, 0, S)
-        nc.vector.quantize_mx(
-            out=z_codes[:].bitcast(FP8X4),
-            scales=z_bytes[:],
-            in_=z_grouped[:].rearrange("p c t -> p (c t)"),
-        )
-        for t in range(PACK):
-            product(h_banks[t][:], w2_codes, w2_bytes, t, z_codes[:], z_bytes[:])
-        difference(2)
+        group_z(1)
+        second_product(1)
+        late_diffs = keep.tile([P, 2, S], F32, name="late_diffs", tag="z_grouped1", align_bytes=64)
+        difference(2, nc.vector)
         make_gate(1, 0, S)
         finish(0, 0, S)
         finish(1, 0, S)
-        difference(3)
+        difference(3, nc.vector)
         make_gate(2, 0, S)
         finish(2, 0, S)
+        last = PACK - 1
         for a in (0, HALF):
             make_gate(last, a, a + HALF)
             finish(last, a, a + HALF)

@@ -79,8 +79,6 @@ def tile_picked_skipjointbgmid_none_p_kernel(
         x_bytes = keep.tile([P, S], U8, name="x_bytes", align_bytes=64)
         nc.vector.tensor_copy(x_bytes[:], scale_table[:].indirect(offs_sb[:]))
 
-        w1_codes = keep.tile([P, H], U32, name="w1_codes", align_bytes=64)
-        w1_bytes = keep.tile([P, H], U8, name="w1_bytes", align_bytes=64)
         w1_view = w1_raw[:].rearrange("p j (m t) -> p m j t", t=PACK)
         w1_pairs = []
         for u in range(2):
@@ -92,13 +90,18 @@ def tile_picked_skipjointbgmid_none_p_kernel(
             else:
                 nc.scalar.activation(dst, src, ACT.Copy)
             w1_pairs.append(pair)
-        for u in range(2):
-            cols = slice(2 * P * u, 2 * P * (u + 1))
+        w1_codes, w1_bytes = {}, {}
+
+        def quantize_w1(u, tag):
+            w1_codes[u] = keep.tile([P, 2 * P], U32, name="w1_codes%d" % u, tag=tag, align_bytes=64)
+            w1_bytes[u] = keep.tile([P, 2 * P], U8, name="w1_bytes%d" % u, align_bytes=64)
             nc.vector.quantize_mx(
-                out=w1_codes[:, cols].bitcast(FP8X4),
-                scales=w1_bytes[:, cols],
+                out=w1_codes[u][:].bitcast(FP8X4),
+                scales=w1_bytes[u][:],
                 in_=w1_pairs[u][:].rearrange("p t m j -> p (t m j)"),
             )
+
+        quantize_w1(0, "w1_codes0")
 
         x_codes = keep.tile([P, S], U32, name="x_codes", align_bytes=64)
         for h in range(2):
@@ -106,6 +109,7 @@ def tile_picked_skipjointbgmid_none_p_kernel(
                 x_codes[:, HALF * h : HALF * (h + 1)],
                 word_table[:].bitcast(U32).indirect(offs_sb[:, HALF // PER_COL * h : HALF // PER_COL * (h + 1)]),
             )
+        quantize_w1(1, "word_table")
 
         def product(bank, codes, scales, t, rhs_codes, rhs_scales):
             rows = slice(P * t, P * (t + 1))
@@ -122,11 +126,11 @@ def tile_picked_skipjointbgmid_none_p_kernel(
         for h in range(2):
             cols = slice(HALF * h, HALF * (h + 1))
             bank = psum.tile([P, HALF], F32, name="first%d" % h, tag="bank%d" % h)
-            product(bank[:], w1_codes, w1_bytes, 0, x_codes[:, cols], x_bytes[:, cols])
+            product(bank[:], w1_codes[0], w1_bytes[0], 0, x_codes[:, cols], x_bytes[:, cols])
             nc.scalar.activation(y[0][:, cols], bank[:], ACT.Copy)
         for t in range(1, PACK):
             bank = psum.tile([P, S], F32, name="ybank%d" % t, tag="bank%d" % (t + 1))
-            product(bank[:], w1_codes, w1_bytes, t, x_codes[:], x_bytes[:])
+            product(bank[:], w1_codes[t // 2], w1_bytes[t // 2], t % 2, x_codes[:], x_bytes[:])
             nc.vector.tensor_copy(y[t][:, :S], bank[:])
 
         w2_grouped = keep.tile([P, PACK, P, PACK], BF16, name="w2_grouped", align_bytes=64)
@@ -280,6 +284,6 @@ def tile_picked_skipjointbgmid_none_p_kernel(
         make_gate(2, 0, S)
         finish(2, 0, S)
         last = PACK - 1
-        for a in (0, HALF):
-            make_gate(last, a, a + HALF)
-            finish(last, a, a + HALF)
+        for a, b in ((0, HALF), (HALF, S - P), (S - P, S)):
+            make_gate(last, a, b)
+            finish(last, a, b)

from contextlib import ExitStack

import concourse.mybir as mybir
from concourse.masks import make_identity

K, T, S, H, N = 512, 2048, 512, 512, 512
MEMBERS = 4

F32 = mybir.dt.float32
BF16 = mybir.dt.bfloat16
I32 = mybir.dt.int32
U32 = mybir.dt.uint32
U16 = mybir.dt.uint16
U8 = mybir.dt.uint8
FP8X4 = mybir.dt.float8_e4m3fn_x4
ALU = mybir.AluOpType
ACT = mybir.ActivationFunctionType

P = 128
PACK = 4
PER_COL = 16
HALF = S // 2
PIECE = 1024
WINDOW = PIECE + PER_COL

FLOPS = 2 * K * H * S + 2 * H * N * S


def tile_picked_skipjointbgmid_none_p_kernel(
    tc, x_words, x_scales, w1, gn, w2, offs, n1, n2, n3, out
):
    nc = tc.nc
    with ExitStack() as ctx:
        lists = ctx.enter_context(tc.tile_pool(name="lists", bufs=1))
        keep = ctx.enter_context(tc.tile_pool(name="keep", bufs=1))
        ring = ctx.enter_context(tc.tile_pool(name="ring", bufs=3))
        psum = ctx.enter_context(tc.psum_pool(name="psum", bufs=1))

        def load_list(name, src):
            tile = lists.tile(list(src.shape), U16, name=name)
            nc.sync.dma_start(tile[:], src)
            return tile

        def load_weight(name, src):
            tile = keep.tile([P, PACK, src.shape[1]], F32, name=name)
            nc.sync.dma_start(tile[:], src.rearrange("(p j) c -> p j c", j=PACK))
            return tile

        scale_table = keep.tile([P, T], U8, name="scale_table", align_bytes=64)
        nc.vector.memset(scale_table[:].bitcast(I32), 0)
        w1_raw = load_weight("w1_raw", w1)
        offs_sb = load_list("offs_sb", offs)
        gain = keep.tile([P, PACK], F32, name="gain")
        nc.sync.dma_start(gain[:], gn.rearrange("(p t) o -> p (t o)", t=PACK))
        for q in range(4):
            nc.sync.dma_start(
                scale_table[32 * q : 32 * q + 4, :].bitcast(I32),
                x_scales[0, 4 * q : 4 * q + 4, :].bitcast(I32),
            )
        word_table = keep.tile([P, T], I32, name="word_table", align_bytes=64)
        nc.sync.dma_start(word_table[:], x_words[0].rearrange("p n t -> p (n t)").bitcast(I32))
        n1_sb = load_list("n1_sb", n1)
        w2_raw = load_weight("w2_raw", w2)
        n2_sb = load_list("n2_sb", n2)
        n3_sb = load_list("n3_sb", n3)

        y = [keep.tile([P, WINDOW], F32, name="y%d" % t) for t in range(PACK)]
        for t in range(PACK):
            nc.vector.memset(y[t][:, S:], 0.0)

        ident = keep.tile([P, P], F32, name="ident")
        make_identity(nc, ident[:])
        gain_bank = psum.tile([P, PACK, P], F32, name="gain_bank", tag="bank5")
        for t in range(PACK):
            nc.tensor.transpose(gain_bank[:, t, :], gain[:, t : t + 1].to_broadcast([P, P]), ident[:])
        gain_row = keep.tile([P, 2, P, 2], F32, name="gain_row")
        nc.scalar.activation(gain_row[:], gain_bank[:].rearrange("j (u e) p -> j u p e", e=2), ACT.Copy)

        x_bytes = keep.tile([P, S], U8, name="x_bytes", align_bytes=64)
        nc.vector.tensor_copy(x_bytes[:], scale_table[:].indirect(offs_sb[:]))

        w1_view = w1_raw[:].rearrange("p j (m t) -> p m j t", t=PACK)
        w1_pairs = []
        for u in range(2):
            pair = keep.tile([P, 2, P, PACK], BF16, name="w1_pair%d" % u, align_bytes=64)
            dst = pair[:].rearrange("p t m j -> p m j t")
            src = w1_view[:, :, :, 2 * u : 2 * u + 2]
            if u == 0:
                nc.vector.tensor_copy(dst, src)
            else:
                nc.scalar.activation(dst, src, ACT.Copy)
            w1_pairs.append(pair)
        w1_codes, w1_bytes = {}, {}

        def quantize_w1(u, tag):
            w1_codes[u] = keep.tile([P, 2 * P], U32, name="w1_codes%d" % u, tag=tag, align_bytes=64)
            w1_bytes[u] = keep.tile([P, 2 * P], U8, name="w1_bytes%d" % u, align_bytes=64)
            nc.vector.quantize_mx(
                out=w1_codes[u][:].bitcast(FP8X4),
                scales=w1_bytes[u][:],
                in_=w1_pairs[u][:].rearrange("p t m j -> p (t m j)"),
            )

        quantize_w1(0, "w1_codes0")

        x_codes = keep.tile([P, S], U32, name="x_codes", align_bytes=64)
        for h in range(2):
            nc.vector.tensor_copy(
                x_codes[:, HALF * h : HALF * (h + 1)],
                word_table[:].bitcast(U32).indirect(offs_sb[:, HALF // PER_COL * h : HALF // PER_COL * (h + 1)]),
            )
        quantize_w1(1, "word_table")

        def product(bank, codes, scales, t, rhs_codes, rhs_scales):
            rows = slice(P * t, P * (t + 1))
            nc.tensor.matmul_mx(
                out=bank,
                lhsT=codes[:, rows].bitcast(FP8X4),
                lhsT_scale=scales[:, rows],
                rhs=rhs_codes.bitcast(FP8X4),
                rhs_scale=rhs_scales,
                start=True,
                stop=True,
            )

        for h in range(2):
            cols = slice(HALF * h, HALF * (h + 1))
            bank = psum.tile([P, HALF], F32, name="first%d" % h, tag="bank%d" % h)
            product(bank[:], w1_codes[0], w1_bytes[0], 0, x_codes[:, cols], x_bytes[:, cols])
            nc.scalar.activation(y[0][:, cols], bank[:], ACT.Copy)
        for t in range(1, PACK):
            bank = psum.tile([P, S], F32, name="ybank%d" % t, tag="bank%d" % (t + 1))
            product(bank[:], w1_codes[t // 2], w1_bytes[t // 2], t % 2, x_codes[:], x_bytes[:])
            nc.vector.tensor_copy(y[t][:, :S], bank[:])

        w2_grouped = keep.tile([P, PACK, P, PACK], BF16, name="w2_grouped", align_bytes=64)
        nc.vector.tensor_copy(
            w2_grouped[:].rearrange("p t m j -> p m j t"),
            w2_raw[:].rearrange("p j (m t) -> p m j t", t=PACK),
        )
        w2_codes = keep.tile([P, N], U32, name="w2_codes", align_bytes=64)
        w2_bytes = keep.tile([P, N], U8, name="w2_bytes", align_bytes=64)

        def quantize_w2():
            nc.vector.quantize_mx(
                out=w2_codes[:].bitcast(FP8X4),
                scales=w2_bytes[:],
                in_=w2_grouped[:].rearrange("p t m j -> p (t m j)"),
            )

        members = {}
        for h in range(2):
            for t in range(PACK):
                mb = keep.tile([P, HALF, MEMBERS], F32, name="mb%d_%d" % (h, t))
                nc.scalar.activation(
                    mb[:].rearrange("p c e -> p (c e)"),
                    y[t][:].indirect(n1_sb[:, PIECE // PER_COL * h : PIECE // PER_COL * (h + 1)]),
                    ACT.Copy,
                    scale=-0.5,
                )
                members[h, t] = mb

        units = [(h, u) for h in range(2) for u in range(2)]
        lows = {k: keep.tile([P, 2, HALF, 2], F32, name="low%d_%d" % k) for k in units}
        highs = {k: keep.tile([P, 2, HALF, 2], F32, name="high%d_%d" % k) for k in units}
        smallest = {k: keep.tile([P, 2, HALF], F32, name="smallest%d_%d" % k) for k in units}
        largest = {k: keep.tile([P, 2, HALF], F32, name="largest%d_%d" % k) for k in units}
        larger = {k: keep.tile([P, 2, HALF], F32, name="larger%d_%d" % k) for k in units}
        sum_tags = ["bank5", "bank6", "bank7", "bank0"]
        sum_banks, word_banks, h_banks = {}, {}, {}
        z_turned = [keep.tile([P, 2, P, 2], BF16, name="z_turned%d" % b) for b in range(4)]
        z_grouped = [keep.tile([P, HALF, PACK], BF16, name="z_grouped%d" % h, align_bytes=64) for h in range(2)]
        z_codes = [keep.tile([P, HALF], U32, name="z_codes%d" % h, align_bytes=64) for h in range(2)]
        z_bytes = [keep.tile([P, HALF], U8, name="z_bytes%d" % h, align_bytes=64) for h in range(2)]

        def pair_step(h, t):
            mb = members[h, t]
            k, e = (h, t // 2), t % 2
            nc.vector.tensor_tensor(highs[k][:, e], mb[:, :, 0:2], mb[:, :, 2:4], ALU.max)
            nc.vector.tensor_tensor(lows[k][:, e], mb[:, :, 0:2], mb[:, :, 2:4], ALU.min)

        def extremes(k):
            nc.vector.tensor_tensor(largest[k][:], highs[k][:, :, :, 0], highs[k][:, :, :, 1], ALU.max)
            nc.vector.tensor_tensor(smallest[k][:], lows[k][:, :, :, 0], lows[k][:, :, :, 1], ALU.min)

        def turn_sums(k):
            h, u = k
            if u == 0:
                for b in (2 * h, 2 * h + 1):
                    sum_banks[b] = psum.tile([P, PACK, P], F32, name="sum_bank%d" % b, tag=sum_tags[b])
            for e in range(2):
                t = 2 * u + e
                nc.vector.scalar_tensor_tensor(
                    larger[k][:, e], largest[k][:, e], -2.0, y[t][:, HALF * h : HALF * (h + 1)], ALU.mult, ALU.max
                )
                for b in range(2):
                    cols = slice(P * b, P * (b + 1))
                    dst = sum_banks[2 * h + b][:, t, :]
                    nc.tensor.matmul(dst, smallest[k][:, e, cols], ident[:], start=True, stop=False, is_transpose=True)
                    nc.tensor.matmul(dst, larger[k][:, e, cols], ident[:], start=False, stop=True, is_transpose=True)

        def gain_and_turn_back(h):
            word_banks[h] = psum.tile([P, 2, 2, P], F32, name="word_bank%d" % h, tag="bank%d" % (1 + h))
            for b in range(2):
                zt = z_turned[2 * h + b]
                nc.vector.tensor_tensor(
                    zt[:], sum_banks[2 * h + b][:].rearrange("j (u e) p -> j u p e", e=2), gain_row[:], ALU.mult
                )
                words = zt[:].rearrange("j u p e -> j (u p e)").bitcast(F32)
                for u in range(2):
                    nc.tensor.transpose(word_banks[h][:, b, u, :], words[:, P * u : P * (u + 1)], ident[:])

        def group_z(h):
            nc.vector.tensor_copy(
                z_grouped[h][:].rearrange("p c t -> p (c t)").bitcast(F32).rearrange("p (b j u) -> p b j u", b=2, u=2),
                word_banks[h][:].rearrange("p b u j -> p b j u"),
            )

        def second_product(h):
            nc.vector.quantize_mx(
                out=z_codes[h][:].bitcast(FP8X4),
                scales=z_bytes[h][:],
                in_=z_grouped[h][:].rearrange("p c t -> p (c t)"),
            )
            for t in range(PACK):
                if h == 0:
                    h_banks[t] = psum.tile([P, S], F32, name="hbank%d" % t, tag="bank%d" % (3 + t))
                product(h_banks[t][:, HALF * h : HALF * (h + 1)], w2_codes, w2_bytes, t, z_codes[h][:], z_bytes[h][:])

        out_rows = out.rearrange("(p t) n -> p t n", t=PACK)
        diffs, gates = {}, {}

        def difference(t, engine):
            g2 = ring.tile([P, S], F32, name="g2")
            g3 = ring.tile([P, S], F32, name="g3")
            nc.scalar.activation(g2[:], y[t][:].indirect(n2_sb[:]), ACT.Copy)
            nc.scalar.activation(g3[:], y[t][:].indirect(n3_sb[:]), ACT.Copy)
            dst = g2[:] if t < 2 else late_diffs[:, t - 2, :]
            engine.tensor_tensor(dst, g2[:], g3[:], ALU.subtract)
            diffs[t] = dst

        def make_gate(t, a, b):
            gate = keep.tile([P, b - a], F32, name="gate%d_%d" % (t, a))
            nc.scalar.activation(gate[:], diffs[t][:, a:b], ACT.Tanh)
            gates[t, a] = gate

        def finish(t, a, b):
            res = keep.tile([P, b - a], F32, name="res%d_%d" % (t, a))
            nc.vector.tensor_tensor(res[:], h_banks[t][:, a:b], gates[t, a][:], ALU.mult)
            nc.sync.dma_start(out_rows[:, t, a:b], res[:])

        pair_step(0, 0)
        quantize_w2()
        pair_step(0, 1)
        extremes((0, 0))
        turn_sums((0, 0))
        pair_step(0, 2)
        pair_step(0, 3)
        extremes((0, 1))
        turn_sums((0, 1))
        pair_step(1, 0)
        gain_and_turn_back(0)
        pair_step(1, 1)
        group_z(0)
        extremes((1, 0))
        second_product(0)
        turn_sums((1, 0))
        pair_step(1, 2)
        pair_step(1, 3)
        extremes((1, 1))
        turn_sums((1, 1))
        difference(0, nc.vector)
        gain_and_turn_back(1)
        difference(1, nc.vector)
        make_gate(0, 0, S)
        group_z(1)
        second_product(1)
        late_diffs = keep.tile([P, 2, S], F32, name="late_diffs", tag="z_grouped1", align_bytes=64)
        difference(2, nc.vector)
        make_gate(1, 0, S)
        finish(0, 0, S)
        finish(1, 0, S)
        difference(3, nc.vector)
        make_gate(2, 0, S)
        finish(2, 0, S)
        last = PACK - 1
        for a, b in ((0, HALF), (HALF, S - P), (S - P, S)):
            make_gate(last, a, b)
            finish(last, a, b)
